import numpy as np
import ml_dtypes


def mxq(x, axis, fmt="e4m3"):
    dtype, down = {"e4m3": (ml_dtypes.float8_e4m3fn, 7), "e5m2": (ml_dtypes.float8_e5m2, 14)}[fmt]
    v = np.moveaxis(np.asarray(x, np.float32).astype(ml_dtypes.bfloat16).astype(np.float64), axis, -1)
    blocks = v.reshape(v.shape[:-1] + (-1, 32))
    amax = np.abs(blocks).max(-1, keepdims=True)
    byte = np.maximum(np.where(amax > 0, np.frexp(amax)[1] - 1 + 127, 0) - down, 1)
    scale = np.exp2(byte - 127.0)
    codes = (blocks / scale).astype(np.float32).astype(dtype).astype(np.float64)
    return np.moveaxis((codes * scale).reshape(v.shape), -1, axis)


WIDE = False


def mx_kscale(k):
    if not WIDE:
        return np.ones(k)
    levels = np.array([10, -10, 5, -5, 0])
    if k % 512:
        return np.exp2(np.random.permutation(np.resize(levels, k // 32))).repeat(32)
    a = np.empty((k // 512, 16))
    for p in range(k // 512):
        a[p, :8] = np.random.permutation(np.resize(levels, 8))
        for g in range(8):
            far = levels[np.abs(levels - a[p, g]) >= 10]
            a[p, g + 8] = far[np.random.randint(len(far))]
    return np.exp2(a.ravel()).repeat(32)


def f64(x):
    return np.asarray(x).astype(np.float64)


def striped(idx):
    return np.tile(np.asarray(idx).reshape(-1, 16).T, (8, 1)).astype(np.uint16)


def unstriped(offs):
    return offs[:16].T.reshape(-1).astype(np.int64)


E2M1 = np.array([0.0, 0.5, 1.0, 1.5, 2.0, 3.0, 4.0, 6.0, -0.0, -0.5, -1.0, -1.5, -2.0, -3.0, -4.0, -6.0])


def pack_weight(w, fmt):
    k, n = w.shape
    w = f64(np.asarray(w, np.float32).astype(ml_dtypes.bfloat16)).reshape(k // 32, 32, n)
    amax = np.abs(w).max(1)
    if fmt == "e4m3":
        byte = np.frexp(amax)[1] - 1 + 127 - 7
    else:
        mant, ex = np.frexp(amax / 6.0)
        byte = np.where(mant > 0.5, ex, ex - 1) + 127
    byte = np.clip(np.where(amax > 0, byte, 1), 1, 254)
    scaled = (w * np.exp2(127.0 - byte)[:, None, :]).reshape(k, n).astype(np.float32)
    by_word = np.ascontiguousarray(scaled.reshape(k // 512, 128, 4, n).transpose(0, 1, 3, 2))
    if fmt == "e4m3":
        words = by_word.astype(ml_dtypes.float8_e4m3fn).view(np.uint8)
    else:
        c = by_word.astype(ml_dtypes.float4_e2m1fn).view(np.uint8) & 0xF
        words = (c[..., 0::2] | (c[..., 1::2] << 4)).reshape(k // 512, 128, 2 * n)
    return np.ascontiguousarray(words), np.ascontiguousarray(byte.astype(np.uint8).reshape(k // 512, 16, n))


def unpack_weight(words, scales, fmt):
    g, _, n = scales.shape
    words = np.ascontiguousarray(words).reshape(g, 128, n, -1)
    if fmt == "e4m3":
        vals = words.view(ml_dtypes.float8_e4m3fn).astype(np.float64)
    else:
        nib = np.empty((g, 128, n, 4), np.uint8)
        nib[..., 0::2] = words & 0xF
        nib[..., 1::2] = words >> 4
        vals = E2M1[nib]
    vals = vals * np.repeat(np.exp2(scales.astype(np.float64) - 127.0), 8, axis=1)[..., None]
    return vals.transpose(0, 1, 3, 2).reshape(g * 512, n)


D, K, V, I, T, Q = 512, 512, 2048, 512, 2048, 128


def setup_inputs():
    n = np.random.standard_normal
    idx = np.random.permutation(T)[:I]
    idx2 = np.random.permutation(V)[:I]
    fd = mx_kscale(D)
    fk = mx_kscale(K)
    embp = pack_weight(n((K, T)) / fk[:, None], "e4m3")
    return {
        "ht": (n((D, Q)) * 1.0 / np.sqrt(D) * fd[:, None]).astype(np.float32),
        "hd": (n((K, Q)) * 1.0 / np.sqrt(K) * fk[:, None]).astype(np.float32),
        "voc": (n((D, V)) / fd[:, None]).astype(np.float32),
        "emb_words": embp[0],
        "emb_scales": embp[1],
        "dw": (np.random.uniform(0.1, 0.4, (Q, 1))).astype(np.float32),
        "offs": striped(idx),
        "offs2": striped(idx2),
    }


def reference(ht, hd, voc, emb_words, emb_scales, dw, offs, offs2):
    idx = unstriped(offs)
    idx2 = unstriped(offs2)
    embu = unpack_weight(emb_words, emb_scales, "e4m3")
    htq = mxq(f64(ht), 0, "e4m3")
    vocq = mxq(f64(voc), 0, "e4m3")
    a = htq.T @ vocq
    hdq = mxq(f64(hd), 0, "e4m3")
    embidxg = embu[:, idx]
    b = hdq.T @ embidxg
    p = np.exp(a - np.max(a, axis=1, keepdims=True))
    r = np.exp(b - np.max(b, axis=1, keepdims=True))
    rn = r * f64(dw) / np.sum(r, axis=1, keepdims=True)
    rf = np.zeros((Q, V))
    rf[:, idx2] = rn
    u = np.maximum(p / np.sum(p, axis=1, keepdims=True) - rf, 0.0)
    y = u / np.sum(u, axis=1, keepdims=True) * 2048.0
    return y

@@ -1,0 +1,245 @@
+from contextlib import ExitStack
+
+import concourse.mybir as mybir
+
+F32 = mybir.dt.float32
+BF16 = mybir.dt.bfloat16
+I32 = mybir.dt.int32
+U32 = mybir.dt.uint32
+U16 = mybir.dt.uint16
+U8 = mybir.dt.uint8
+FP8X4 = mybir.dt.float8_e4m3fn_x4
+ALU = mybir.AluOpType
+ACT = mybir.ActivationFunctionType
+
+P = 128
+PACK = 4
+Q = 128
+V = 2048
+T = 2048
+I = 512
+WIDTHS = (512, 512, 256, 256, 256, 256)
+LOADS = (256,) * 8
+TINY = 1e-26
+CAST = 256
+
+FLOPS = 2 * 512 * Q * (V + I)
+
+
+def interleave(engine_copy, dst, src):
+    engine_copy(
+        out=dst.rearrange("p (c i) t -> p c t i", i=4),
+        in_=src.rearrange("p t (c i) -> p c t i", i=4),
+    )
+
+
+def tile_attend_shortvocab_kernel(tc, ht, hd, voc, emb_words, emb_scales, dw, offs, offs2, out):
+    nc = tc.nc
+    n_chunks = len(WIDTHS)
+    last = n_chunks - 1
+    starts = [sum(WIDTHS[:c]) for c in range(n_chunks)]
+
+    with ExitStack() as ctx:
+        keep = ctx.enter_context(tc.tile_pool(name="keep", bufs=1))
+        psum = ctx.enter_context(tc.psum_pool(name="psum", bufs=1))
+
+        def sb(shape, dtype, name, tag=None):
+            return keep.tile(shape, dtype, name=name, tag=tag or name, align_bytes=64)
+
+        offs_sb = sb([P, I // 16], U16, "offs_sb")
+        offs2_sb = sb([P, I // 16], U16, "offs2_sb")
+        dw_sb = sb([P, 1], F32, "dw_sb")
+        words = sb([P, T], U32, "words")
+        scales = sb([P, T], U8, "scales", "scales_then_words")
+        hd_raw = sb([P, PACK, Q], F32, "hd_raw")
+        ht_raw = sb([P, PACK, Q], F32, "ht_raw")
+        voc_raw = [sb([P, PACK, w], F32, "voc_raw%d" % c) for c, w in enumerate(LOADS)]
+        load_starts = [sum(LOADS[:c]) for c in range(len(LOADS))]
+        rf = sb([P, V], F32, "rf")
+        warm = sb([P, 1], F32, "warm")
+        warm_out = sb([P, 1], F32, "warm_out")
+        e = sb([P, n_chunks], F32, "e")
+
+        nc.vector.memset(scales[:].bitcast(I32), 0)
+        nc.vector.memset(warm[:], 0.0)
+        nc.vector.memset(e[:, last:], 1.0)
+        nc.vector.memset(rf[:], 0.0)
+
+        def load_voc(c):
+            cols = slice(load_starts[c], load_starts[c] + LOADS[c])
+            nc.sync.dma_start(out=voc_raw[c][:], in_=voc[:, cols].rearrange("(p j) w -> p j w", j=PACK))
+
+        nc.sync.dma_start(out=offs_sb[:], in_=offs)
+        nc.sync.dma_start(out=offs2_sb[:], in_=offs2)
+        nc.sync.dma_start(out=hd_raw[:], in_=hd.rearrange("(p j) w -> p j w", j=PACK))
+        nc.sync.dma_start(out=words[:].bitcast(I32), in_=emb_words[0].rearrange("p n t -> p (n t)").bitcast(I32))
+        for g in range(4):
+            nc.scalar.dma_start(
+                out=scales[:].bitcast(I32)[32 * g : 32 * g + 4, :],
+                in_=emb_scales[0, 4 * g : 4 * g + 4, :].bitcast(I32),
+            )
+        nc.scalar.activation(out=warm_out[:], in_=warm[:], func=ACT.Exp)
+        load_voc(0)
+        load_voc(1)
+        nc.sync.dma_start(out=ht_raw[:], in_=ht.rearrange("(p j) w -> p j w", j=PACK))
+        nc.sync.dma_start(out=dw_sb[:], in_=dw)
+        for c in range(2, len(LOADS)):
+            load_voc(c)
+
+        hd_bf = sb([P, Q, PACK], BF16, "hd_bf")
+        ht_bf = sb([P, Q, PACK], BF16, "ht_bf")
+        voc_bf = [sb([P, w, PACK], BF16, "voc_bf%d" % c) for c, w in enumerate(WIDTHS)]
+
+        def cast_voc(col, width, engine_copy):
+            c = max(i for i in range(n_chunks) if starts[i] <= col)
+            ld = max(i for i in range(len(LOADS)) if load_starts[i] <= col)
+            a, b0 = col - starts[c], col - load_starts[ld]
+            interleave(engine_copy, voc_bf[c][:, a : a + width, :], voc_raw[ld][:, :, b0 : b0 + width])
+
+        def quantize(src, width, name):
+            codes = sb([P, width], U32, name + "_codes")
+            plane = sb([P, width], U8, name + "_plane")
+            nc.vector.quantize_mx(
+                out=codes[:].bitcast(FP8X4), scales=plane[:], in_=src[:].rearrange("p w t -> p (w t)")
+            )
+            return codes, plane
+
+        def product(lhs, codes, plane, width, name):
+            bank = psum.tile([P, width], F32, name=name)
+            nc.tensor.matmul_mx(
+                out=bank[:],
+                lhsT=lhs[0][:].bitcast(FP8X4),
+                lhsT_scale=lhs[1][:],
+                rhs=codes.bitcast(FP8X4),
+                rhs_scale=plane,
+                start=True,
+                stop=True,
+            )
+            return bank
+
+        def negate_and_min(dst, bank, low, before):
+            nc.vector.tensor_scalar(
+                out=dst, in0=bank[:], scalar1=-1.0, scalar2=before, op0=ALU.mult, op1=ALU.min, accum_out=low
+            )
+
+        def exponentials(dst, neg, low, total):
+            nc.scalar.activation(out=dst, in_=neg, func=ACT.Exp, bias=low, scale=-1.0, accum_out=total)
+
+        nm = sb([P, n_chunks], F32, "nm")
+        s = voc_raw[7][:, 0, 0:n_chunks]
+        p = sb([P, V], F32, "p")
+        banks = {}
+        span = [slice(starts[c], starts[c] + WIDTHS[c]) for c in range(n_chunks)]
+
+        def scores(c):
+            codes, plane = quantize(voc_bf[c], WIDTHS[c], "voc%d" % c)
+            banks[c] = product(ht_q, codes[:], plane[:], WIDTHS[c], "a%d" % c)
+
+        half = I // 2
+        halves = [slice(0, half), slice(half, I)]
+        lists = [slice(0, half // 16), slice(half // 16, I // 16)]
+        interleave(nc.scalar.copy, hd_bf[:], hd_raw[:])
+        hd_q = quantize(hd_bf, Q, "hd")
+        g_scales = sb([P, I], U8, "g_scales")
+        nc.vector.tensor_copy(out=g_scales[:], in_=scales[:].indirect(offs_sb[:]))
+        g_words = sb([P, I], U32, "g_words", "scales_then_words")
+        for h in range(2):
+            nc.vector.tensor_copy(out=g_words[:, halves[h]], in_=words[:].indirect(offs_sb[:, lists[h]]))
+        b = [product(hd_q, g_words[:, halves[h]], g_scales[:, halves[h]], half, "b%d" % h) for h in range(2)]
+        first = sb([P, I], F32, "first")
+        neg_b1 = sb([P, half], F32, "neg_b1")
+        neg_b = [first[:, :half], neg_b1[:]]
+        neg_last = sb([P, WIDTHS[last]], F32, "neg_last")
+        flat = [raw[:].rearrange("p j w -> p (j w)") for raw in voc_raw]
+        neg_a = [first[:], flat[4][:, :512], flat[5][:, :256], flat[6][:, :256], flat[7][:, 256:512], neg_last[:]]
+        nb = sb([P, 2], F32, "nb")
+        negate_and_min(neg_b[0], b[0], nb[:, 0:1], None)
+        negate_and_min(neg_b[1], b[1], nb[:, 1:2], nb[:, 0:1])
+        r_part = sb([P, 2], F32, "r_part")
+        r0 = sb([P, half], F32, "r0")
+        r = [r0[:], voc_raw[3][:, 0, :]]
+
+        def draft_weights(h):
+            exponentials(r[h], neg_b[h], nb[:, 1:2], r_part[:, h : h + 1])
+
+        def scatter(h):
+            nc.vector.tensor_copy(out=rf[:].indirect(offs2_sb[:, lists[h]]), in_=r[h])
+
+        draft_weights(0)
+        scatter(0)
+        cast_voc(0, CAST, nc.scalar.copy)
+        cast_voc(CAST, CAST, nc.scalar.copy)
+        interleave(nc.vector.tensor_copy, ht_bf[:], ht_raw[:])
+        ht_q = quantize(ht_bf, Q, "ht")
+        scores(0)
+        cast_voc(2 * CAST, CAST, nc.scalar.copy)
+        cast_voc(3 * CAST, CAST, nc.scalar.copy)
+        draft_weights(1)
+        for unit in range(4, 7):
+            cast_voc(unit * CAST, CAST, nc.scalar.copy)
+        cast_voc(7 * CAST, CAST // 2, nc.scalar.copy)
+        cast_voc(7 * CAST + CAST // 2, CAST // 2, nc.vector.tensor_copy)
+        scores(1)
+        scatter(1)
+        for c in range(2, n_chunks):
+            scores(c)
+        for c in range(n_chunks):
+            negate_and_min(neg_a[c], banks[c], nm[:, c : c + 1], nm[:, c - 1 : c] if c else None)
+
+        r_sum = sb([P, 1], F32, "r_sum")
+        nc.gpsimd.tensor_tensor(out=r_sum[:], in0=r_part[:, 0:1], in1=r_part[:, 1:2], op=ALU.add)
+        r_inv = sb([P, 1], F32, "r_inv")
+        nc.vector.reciprocal(out=r_inv[:], in_=r_sum[:])
+        neg_c = sb([P, 1], F32, "neg_c")
+        nc.gpsimd.tensor_scalar(
+            out=neg_c[:], in0=r_inv[:], scalar1=dw_sb[:], scalar2=-1.0, op0=ALU.mult, op1=ALU.mult
+        )
+
+        for c in range(last):
+            exponentials(p[:, span[c]], neg_a[c], nm[:, c : c + 1], s[:, c : c + 1])
+        e_raw = sb([P, last], F32, "e_raw")
+        nc.scalar.activation(out=e_raw[:], in_=nm[:, :last], func=ACT.Exp, bias=nm[:, last:], scale=-1.0)
+        exponentials(p[:, span[last]], neg_a[last], nm[:, last:], s[:, last:])
+        nc.vector.tensor_scalar(out=e[:, :last], in0=e_raw[:], scalar1=TINY, scalar2=None, op0=ALU.max)
+        g = sb([P, last], F32, "g")
+        nc.vector.reciprocal(out=g[:], in_=e[:, :last])
+
+        es = sb([P, n_chunks], F32, "es")
+        t = sb([P, n_chunks], F32, "t")
+        nc.vector.scalar_tensor_tensor(
+            out=es[:], in0=s, scalar=neg_c[:], in1=e[:], op0=ALU.mult, op1=ALU.mult, accum_out=t[:, last:]
+        )
+        nc.vector.tensor_scalar(out=t[:, :last], in0=g[:], scalar1=t[:, last:], scalar2=None, op0=ALU.mult)
+
+        d = sb([P, V], F32, "d")
+        u = sb([P, V], F32, "u")
+        u_part = sb([P, n_chunks], F32, "u_part")
+        order = [5, 2, 3, 0, 1, 4]
+        for c in order:
+            cols = span[c]
+            nc.vector.scalar_tensor_tensor(
+                out=d[:, cols], in0=rf[:, cols], scalar=t[:, c : c + 1], in1=p[:, cols], op0=ALU.mult, op1=ALU.add
+            )
+            if c != order[-1]:
+                nc.scalar.activation(out=u[:, cols], in_=d[:, cols], func=ACT.Relu, accum_out=u_part[:, c : c + 1])
+            else:
+                nc.vector.tensor_scalar(
+                    out=u[:, cols], in0=d[:, cols], scalar1=0.0, scalar2=None, op0=ALU.max, op1=ALU.add,
+                    accum_out=u_part[:, c : c + 1],
+                )
+        u_scaled = sb([P, n_chunks], F32, "u_scaled")
+        u_sum = sb([P, 1], F32, "u_sum")
+        nc.vector.scalar_tensor_tensor(
+            out=u_scaled[:], in0=u_part[:], scalar=1.0 / V, in1=e[:], op0=ALU.mult, op1=ALU.mult, accum_out=u_sum[:]
+        )
+        k = sb([P, 1], F32, "k")
+        nc.vector.reciprocal(out=k[:], in_=u_sum[:])
+        y = sb([P, V], F32, "y")
+        for group in ((5,), (4,), (0,), (1,), (2, 3)):
+            for c in group:
+                nc.vector.tensor_scalar(
+                    out=y[:, span[c]], in0=u[:, span[c]], scalar1=k[:], scalar2=e[:, c : c + 1],
+                    op0=ALU.mult, op1=ALU.mult,
+                )
+            cols = slice(span[group[0]].start, span[group[-1]].stop)
+            nc.sync.dma_start(out=out[:, cols], in_=y[:, cols])

@@ -18,9 +18,10 @@ Q = 128
 V = 2048
 T = 2048
 I = 512
-WIDTHS = (512, 512, 256, 256, 256, 256)
-LOADS = (256,) * 8
+WIDTHS = (256, 512, 512, 512, 256)
+LOADS = WIDTHS
 TINY = 1e-26
+ON_VECTOR = 384
 CAST = 256
 
 FLOPS = 2 * 512 * Q * (V + I)
@@ -59,10 +60,13 @@ def tile_attend_shortvocab_kernel(tc, ht, hd, voc, emb_words, emb_scales, dw, of
         warm = sb([P, 1], F32, "warm")
         warm_out = sb([P, 1], F32, "warm_out")
         e = sb([P, n_chunks], F32, "e")
+        weight = sb([P, n_chunks + 1], F32, "weight")
+        u_part = sb([P, n_chunks + 1], F32, "u_part")
 
         nc.vector.memset(scales[:].bitcast(I32), 0)
         nc.vector.memset(warm[:], 0.0)
         nc.vector.memset(e[:, last:], 1.0)
+        nc.vector.memset(weight[:, :n_chunks], 1.0)
         nc.vector.memset(rf[:], 0.0)
 
         def load_voc(c):
@@ -80,8 +84,8 @@ def tile_attend_shortvocab_kernel(tc, ht, hd, voc, emb_words, emb_scales, dw, of
             )
         nc.scalar.activation(out=warm_out[:], in_=warm[:], func=ACT.Exp)
         load_voc(0)
-        load_voc(1)
         nc.sync.dma_start(out=ht_raw[:], in_=ht.rearrange("(p j) w -> p j w", j=PACK))
+        load_voc(1)
         nc.sync.dma_start(out=dw_sb[:], in_=dw)
         for c in range(2, len(LOADS)):
             load_voc(c)
@@ -126,7 +130,7 @@ def tile_attend_shortvocab_kernel(tc, ht, hd, voc, emb_words, emb_scales, dw, of
             nc.scalar.activation(out=dst, in_=neg, func=ACT.Exp, bias=low, scale=-1.0, accum_out=total)
 
         nm = sb([P, n_chunks], F32, "nm")
-        s = voc_raw[7][:, 0, 0:n_chunks]
+        s = voc_raw[last][:, 0, 0:n_chunks]
         p = sb([P, V], F32, "p")
         banks = {}
         span = [slice(starts[c], starts[c] + WIDTHS[c]) for c in range(n_chunks)]
@@ -146,52 +150,36 @@ def tile_attend_shortvocab_kernel(tc, ht, hd, voc, emb_words, emb_scales, dw, of
         for h in range(2):
             nc.vector.tensor_copy(out=g_words[:, halves[h]], in_=words[:].indirect(offs_sb[:, lists[h]]))
         b = [product(hd_q, g_words[:, halves[h]], g_scales[:, halves[h]], half, "b%d" % h) for h in range(2)]
-        first = sb([P, I], F32, "first")
-        neg_b1 = sb([P, half], F32, "neg_b1")
-        neg_b = [first[:, :half], neg_b1[:]]
+        neg_b = sb([P, I], F32, "neg_b")
         neg_last = sb([P, WIDTHS[last]], F32, "neg_last")
         flat = [raw[:].rearrange("p j w -> p (j w)") for raw in voc_raw]
-        neg_a = [first[:], flat[4][:, :512], flat[5][:, :256], flat[6][:, :256], flat[7][:, 256:512], neg_last[:]]
+        neg_a = [neg_b[:, :256], flat[2][:, :512], flat[3][:, :512], flat[4][:, 256:768], neg_last[:]]
         nb = sb([P, 2], F32, "nb")
-        negate_and_min(neg_b[0], b[0], nb[:, 0:1], None)
-        negate_and_min(neg_b[1], b[1], nb[:, 1:2], nb[:, 0:1])
-        r_part = sb([P, 2], F32, "r_part")
-        r0 = sb([P, half], F32, "r0")
-        r = [r0[:], voc_raw[3][:, 0, :]]
-
-        def draft_weights(h):
-            exponentials(r[h], neg_b[h], nb[:, 1:2], r_part[:, h : h + 1])
-
-        def scatter(h):
-            nc.vector.tensor_copy(out=rf[:].indirect(offs2_sb[:, lists[h]]), in_=r[h])
-
-        draft_weights(0)
-        scatter(0)
-        cast_voc(0, CAST, nc.scalar.copy)
-        cast_voc(CAST, CAST, nc.scalar.copy)
-        interleave(nc.vector.tensor_copy, ht_bf[:], ht_raw[:])
+        negate_and_min(neg_b[:, halves[0]], b[0], nb[:, 0:1], None)
+        negate_and_min(neg_b[:, halves[1]], b[1], nb[:, 1:2], nb[:, 0:1])
+        r = sb([P, I], F32, "r")
+        r_sum = sb([P, 1], F32, "r_sum")
+        exponentials(r[:], neg_b[:], nb[:, 1:2], r_sum[:])
+        interleave(nc.scalar.copy, ht_bf[:], ht_raw[:])
         ht_q = quantize(ht_bf, Q, "ht")
+        cast_voc(0, CAST, nc.scalar.copy)
         scores(0)
-        cast_voc(2 * CAST, CAST, nc.scalar.copy)
-        cast_voc(3 * CAST, CAST, nc.scalar.copy)
-        draft_weights(1)
-        for unit in range(4, 7):
+        nc.vector.tensor_copy(out=rf[:].indirect(offs2_sb[:]), in_=r[:])
+        negate_and_min(neg_a[0], banks[0], nm[:, 0:1], None)
+        for unit in (1, 2, 3, 5, 7):
             cast_voc(unit * CAST, CAST, nc.scalar.copy)
-        cast_voc(7 * CAST, CAST // 2, nc.scalar.copy)
-        cast_voc(7 * CAST + CAST // 2, CAST // 2, nc.vector.tensor_copy)
         scores(1)
-        scatter(1)
+        for unit in (4, 6):
+            cast_voc(unit * CAST, CAST, nc.vector.tensor_copy)
         for c in range(2, n_chunks):
             scores(c)
-        for c in range(n_chunks):
-            negate_and_min(neg_a[c], banks[c], nm[:, c : c + 1], nm[:, c - 1 : c] if c else None)
+        for c in range(1, n_chunks):
+            negate_and_min(neg_a[c], banks[c], nm[:, c : c + 1], nm[:, c - 1 : c])
 
-        r_sum = sb([P, 1], F32, "r_sum")
-        nc.gpsimd.tensor_tensor(out=r_sum[:], in0=r_part[:, 0:1], in1=r_part[:, 1:2], op=ALU.add)
-        r_inv = sb([P, 1], F32, "r_inv")
+        r_inv = sb([P, 1], F32, "r_inv", "voc%d_plane" % last)
         nc.vector.reciprocal(out=r_inv[:], in_=r_sum[:])
         neg_c = sb([P, 1], F32, "neg_c")
-        nc.gpsimd.tensor_scalar(
+        nc.vector.tensor_scalar(
             out=neg_c[:], in0=r_inv[:], scalar1=dw_sb[:], scalar2=-1.0, op0=ALU.mult, op1=ALU.mult
         )
 
@@ -201,6 +189,9 @@ def tile_attend_shortvocab_kernel(tc, ht, hd, voc, emb_words, emb_scales, dw, of
         nc.scalar.activation(out=e_raw[:], in_=nm[:, :last], func=ACT.Exp, bias=nm[:, last:], scale=-1.0)
         exponentials(p[:, span[last]], neg_a[last], nm[:, last:], s[:, last:])
         nc.vector.tensor_scalar(out=e[:, :last], in0=e_raw[:], scalar1=TINY, scalar2=None, op0=ALU.max)
+        nc.vector.tensor_scalar(
+            out=weight[:, n_chunks:], in0=e_raw[:, last - 1 :], scalar1=TINY, scalar2=None, op0=ALU.max
+        )
         g = sb([P, last], F32, "g")
         nc.vector.reciprocal(out=g[:], in_=e[:, :last])
 
@@ -213,33 +204,43 @@ def tile_attend_shortvocab_kernel(tc, ht, hd, voc, emb_words, emb_scales, dw, of
 
         d = sb([P, V], F32, "d")
         u = sb([P, V], F32, "u")
-        u_part = sb([P, n_chunks], F32, "u_part")
-        order = [5, 2, 3, 0, 1, 4]
-        for c in order:
-            cols = span[c]
+        mid = starts[last - 1] + ON_VECTOR
+        own = slice(starts[last - 1], mid)
+
+        def differences(c, cols):
             nc.vector.scalar_tensor_tensor(
                 out=d[:, cols], in0=rf[:, cols], scalar=t[:, c : c + 1], in1=p[:, cols], op0=ALU.mult, op1=ALU.add
             )
-            if c != order[-1]:
-                nc.scalar.activation(out=u[:, cols], in_=d[:, cols], func=ACT.Relu, accum_out=u_part[:, c : c + 1])
-            else:
-                nc.vector.tensor_scalar(
-                    out=u[:, cols], in0=d[:, cols], scalar1=0.0, scalar2=None, op0=ALU.max, op1=ALU.add,
-                    accum_out=u_part[:, c : c + 1],
-                )
-        u_scaled = sb([P, n_chunks], F32, "u_scaled")
+
+        def positive_parts(c, cols):
+            nc.scalar.activation(
+                out=u[:, cols], in_=d[:, cols], func=ACT.Relu, scale=e[:, c : c + 1], accum_out=u_part[:, c : c + 1]
+            )
+
+        for c in [last] + list(range(last - 1)):
+            differences(c, span[c])
+            positive_parts(c, span[c])
+        differences(last - 1, own)
+        differences(last - 1, slice(mid, starts[last]))
+        positive_parts(last - 1, slice(mid, starts[last]))
+        nc.vector.tensor_scalar(
+            out=u[:, own], in0=d[:, own], scalar1=0.0, scalar2=None, op0=ALU.max, op1=ALU.add,
+            accum_out=u_part[:, n_chunks:],
+        )
+        u_scaled = sb([P, n_chunks + 1], F32, "u_scaled")
         u_sum = sb([P, 1], F32, "u_sum")
         nc.vector.scalar_tensor_tensor(
-            out=u_scaled[:], in0=u_part[:], scalar=1.0 / V, in1=e[:], op0=ALU.mult, op1=ALU.mult, accum_out=u_sum[:]
+            out=u_scaled[:], in0=u_part[:], scalar=1.0 / V, in1=weight[:], op0=ALU.mult, op1=ALU.mult,
+            accum_out=u_sum[:],
         )
         k = sb([P, 1], F32, "k")
         nc.vector.reciprocal(out=k[:], in_=u_sum[:])
         y = sb([P, V], F32, "y")
-        for group in ((5,), (4,), (0,), (1,), (2, 3)):
-            for c in group:
-                nc.vector.tensor_scalar(
-                    out=y[:, span[c]], in0=u[:, span[c]], scalar1=k[:], scalar2=e[:, c : c + 1],
-                    op0=ALU.mult, op1=ALU.mult,
-                )
-            cols = slice(span[group[0]].start, span[group[-1]].stop)
-            nc.sync.dma_start(out=out[:, cols], in_=y[:, cols])
+        for c in range(last - 1):
+            nc.vector.tensor_scalar(out=y[:, span[c]], in0=u[:, span[c]], scalar1=k[:], scalar2=None, op0=ALU.mult)
+            nc.sync.dma_start(out=out[:, span[c]], in_=y[:, span[c]])
+        nc.vector.tensor_scalar(
+            out=y[:, own], in0=u[:, own], scalar1=k[:], scalar2=weight[:, n_chunks:], op0=ALU.mult, op1=ALU.mult
+        )
+        nc.vector.tensor_scalar(out=y[:, mid:], in0=u[:, mid:], scalar1=k[:], scalar2=None, op0=ALU.mult)
+        nc.sync.dma_start(out=out[:, starts[last - 1] :], in_=y[:, starts[last - 1] :])

@@ -21,7 +21,7 @@ I = 512
 WIDTHS = (256, 512, 512, 512, 256)
 LOADS = WIDTHS
 TINY = 1e-26
-ON_VECTOR = 384
+ON_VECTOR = 256
 CAST = 256
 
 FLOPS = 2 * 512 * Q * (V + I)
@@ -86,9 +86,9 @@ def tile_attend_shortvocab_kernel(tc, ht, hd, voc, emb_words, emb_scales, dw, of
         load_voc(0)
         nc.sync.dma_start(out=ht_raw[:], in_=ht.rearrange("(p j) w -> p j w", j=PACK))
         load_voc(1)
-        nc.sync.dma_start(out=dw_sb[:], in_=dw)
         for c in range(2, len(LOADS)):
             load_voc(c)
+        nc.sync.dma_start(out=dw_sb[:], in_=dw)
 
         hd_bf = sb([P, Q, PACK], BF16, "hd_bf")
         ht_bf = sb([P, Q, PACK], BF16, "ht_bf")
@@ -166,11 +166,10 @@ def tile_attend_shortvocab_kernel(tc, ht, hd, voc, emb_words, emb_scales, dw, of
         scores(0)
         nc.vector.tensor_copy(out=rf[:].indirect(offs2_sb[:]), in_=r[:])
         negate_and_min(neg_a[0], banks[0], nm[:, 0:1], None)
-        for unit in (1, 2, 3, 5, 7):
+        for unit in (1, 2, 3, 4, 5, 7):
             cast_voc(unit * CAST, CAST, nc.scalar.copy)
         scores(1)
-        for unit in (4, 6):
-            cast_voc(unit * CAST, CAST, nc.vector.tensor_copy)
+        cast_voc(6 * CAST, CAST, nc.vector.tensor_copy)
         for c in range(2, n_chunks):
             scores(c)
         for c in range(1, n_chunks):

@@ -58,14 +58,12 @@ def tile_attend_shortvocab_kernel(tc, ht, hd, voc, emb_words, emb_scales, dw, of
         load_starts = [sum(LOADS[:c]) for c in range(len(LOADS))]
         rf = sb([P, V], F32, "rf")
         warm = sb([P, 1], F32, "warm")
-        warm_out = sb([P, 1], F32, "warm_out")
         e = sb([P, n_chunks], F32, "e")
         weight = sb([P, n_chunks + 1], F32, "weight")
         u_part = sb([P, n_chunks + 1], F32, "u_part")
 
         nc.vector.memset(scales[:].bitcast(I32), 0)
         nc.vector.memset(warm[:], 0.0)
-        nc.vector.memset(e[:, last:], 1.0)
         nc.vector.memset(weight[:, :n_chunks], 1.0)
         nc.vector.memset(rf[:], 0.0)
 
@@ -82,7 +80,7 @@ def tile_attend_shortvocab_kernel(tc, ht, hd, voc, emb_words, emb_scales, dw, of
                 out=scales[:].bitcast(I32)[32 * g : 32 * g + 4, :],
                 in_=emb_scales[0, 4 * g : 4 * g + 4, :].bitcast(I32),
             )
-        nc.scalar.activation(out=warm_out[:], in_=warm[:], func=ACT.Exp)
+        nc.scalar.activation(out=e[:, last:], in_=warm[:], func=ACT.Exp)
         load_voc(0)
         nc.sync.dma_start(out=ht_raw[:], in_=ht.rearrange("(p j) w -> p j w", j=PACK))
         load_voc(1)

@@ -17,28 +17,33 @@ PACK = 4
 Q = 128
 V = 2048
 T = 2048
-I = 512
-WIDTHS = (256, 512, 512, 512, 256)
-LOADS = WIDTHS
-TINY = 1e-26
-ON_VECTOR = 256
-CAST = 256
+ENTRIES = 512
+PER_COLUMN = 16
+QUADRANT = 32
+LINE = 4
 
-FLOPS = 2 * 512 * Q * (V + I)
+WIDTHS = (256, 512, 512, 512, 256)
+PIECE = 256
+VECTOR_PIECE = V // PIECE - 2
+ON_VECTOR = 256
+TINY = 1e-26
+
+FLOPS = 2 * P * PACK * Q * (V + ENTRIES)
 
 
 def interleave(engine_copy, dst, src):
     engine_copy(
-        out=dst.rearrange("p (c i) t -> p c t i", i=4),
-        in_=src.rearrange("p t (c i) -> p c t i", i=4),
+        out=dst.rearrange("p (c i) t -> p c t i", i=LINE),
+        in_=src.rearrange("p t (c i) -> p c t i", i=LINE),
     )
 
 
 def tile_attend_shortvocab_kernel(tc, ht, hd, voc, emb_words, emb_scales, dw, offs, offs2, out):
     nc = tc.nc
-    n_chunks = len(WIDTHS)
-    last = n_chunks - 1
-    starts = [sum(WIDTHS[:c]) for c in range(n_chunks)]
+    groups = len(WIDTHS)
+    last = groups - 1
+    starts = [sum(WIDTHS[:g]) for g in range(groups)]
+    span = [slice(starts[g], starts[g] + WIDTHS[g]) for g in range(groups)]
 
     with ExitStack() as ctx:
         keep = ctx.enter_context(tc.tile_pool(name="keep", bufs=1))
@@ -47,56 +52,51 @@ def tile_attend_shortvocab_kernel(tc, ht, hd, voc, emb_words, emb_scales, dw, of
         def sb(shape, dtype, name, tag=None):
             return keep.tile(shape, dtype, name=name, tag=tag or name, align_bytes=64)
 
-        offs_sb = sb([P, I // 16], U16, "offs_sb")
-        offs2_sb = sb([P, I // 16], U16, "offs2_sb")
+        offs_sb = sb([P, ENTRIES // PER_COLUMN], U16, "offs_sb")
+        offs2_sb = sb([P, ENTRIES // PER_COLUMN], U16, "offs2_sb")
         dw_sb = sb([P, 1], F32, "dw_sb")
         words = sb([P, T], U32, "words")
         scales = sb([P, T], U8, "scales", "scales_then_words")
         hd_raw = sb([P, PACK, Q], F32, "hd_raw")
         ht_raw = sb([P, PACK, Q], F32, "ht_raw")
-        voc_raw = [sb([P, PACK, w], F32, "voc_raw%d" % c) for c, w in enumerate(LOADS)]
-        load_starts = [sum(LOADS[:c]) for c in range(len(LOADS))]
+        voc_raw = [sb([P, PACK, w], F32, "voc_raw%d" % g) for g, w in enumerate(WIDTHS)]
         rf = sb([P, V], F32, "rf")
-        warm = sb([P, 1], F32, "warm")
-        e = sb([P, n_chunks], F32, "e")
-        weight = sb([P, n_chunks + 1], F32, "weight")
-        u_part = sb([P, n_chunks + 1], F32, "u_part")
+        zero = sb([P, 1], F32, "zero")
+        e = sb([P, 2 * groups - 1], F32, "e")
+        u_part = sb([P, groups + 1], F32, "u_part")
 
         nc.vector.memset(scales[:].bitcast(I32), 0)
-        nc.vector.memset(warm[:], 0.0)
-        nc.vector.memset(weight[:, :n_chunks], 1.0)
+        nc.vector.memset(zero[:], 0.0)
+        nc.vector.memset(e[:, groups:], 1.0)
         nc.vector.memset(rf[:], 0.0)
 
-        def load_voc(c):
-            cols = slice(load_starts[c], load_starts[c] + LOADS[c])
-            nc.sync.dma_start(out=voc_raw[c][:], in_=voc[:, cols].rearrange("(p j) w -> p j w", j=PACK))
+        def load_rows(dst, rows):
+            nc.sync.dma_start(out=dst[:], in_=rows.rearrange("(p j) w -> p j w", j=PACK))
 
         nc.sync.dma_start(out=offs_sb[:], in_=offs)
         nc.sync.dma_start(out=offs2_sb[:], in_=offs2)
-        nc.sync.dma_start(out=hd_raw[:], in_=hd.rearrange("(p j) w -> p j w", j=PACK))
+        load_rows(hd_raw, hd)
         nc.sync.dma_start(out=words[:].bitcast(I32), in_=emb_words[0].rearrange("p n t -> p (n t)").bitcast(I32))
-        for g in range(4):
+        for quad in range(P // QUADRANT):
             nc.scalar.dma_start(
-                out=scales[:].bitcast(I32)[32 * g : 32 * g + 4, :],
-                in_=emb_scales[0, 4 * g : 4 * g + 4, :].bitcast(I32),
+                out=scales[:].bitcast(I32)[QUADRANT * quad : QUADRANT * quad + 4, :],
+                in_=emb_scales[0, 4 * quad : 4 * quad + 4, :].bitcast(I32),
             )
-        nc.scalar.activation(out=e[:, last:], in_=warm[:], func=ACT.Exp)
-        load_voc(0)
-        nc.sync.dma_start(out=ht_raw[:], in_=ht.rearrange("(p j) w -> p j w", j=PACK))
-        load_voc(1)
-        for c in range(2, len(LOADS)):
-            load_voc(c)
+        nc.scalar.activation(out=e[:, last:groups], in_=zero[:], func=ACT.Exp)
+        load_rows(voc_raw[0], voc[:, span[0]])
+        load_rows(ht_raw, ht)
+        for g in range(1, groups):
+            load_rows(voc_raw[g], voc[:, span[g]])
         nc.sync.dma_start(out=dw_sb[:], in_=dw)
 
         hd_bf = sb([P, Q, PACK], BF16, "hd_bf")
         ht_bf = sb([P, Q, PACK], BF16, "ht_bf")
-        voc_bf = [sb([P, w, PACK], BF16, "voc_bf%d" % c) for c, w in enumerate(WIDTHS)]
+        voc_bf = [sb([P, w, PACK], BF16, "voc_bf%d" % g) for g, w in enumerate(WIDTHS)]
 
-        def cast_voc(col, width, engine_copy):
-            c = max(i for i in range(n_chunks) if starts[i] <= col)
-            ld = max(i for i in range(len(LOADS)) if load_starts[i] <= col)
-            a, b0 = col - starts[c], col - load_starts[ld]
-            interleave(engine_copy, voc_bf[c][:, a : a + width, :], voc_raw[ld][:, :, b0 : b0 + width])
+        def interleave_piece(piece, engine_copy):
+            g = max(i for i in range(groups) if starts[i] <= piece * PIECE)
+            cols = slice(piece * PIECE - starts[g], (piece + 1) * PIECE - starts[g])
+            interleave(engine_copy, voc_bf[g][:, cols, :], voc_raw[g][:, :, cols])
 
         def quantize(src, width, name):
             codes = sb([P, width], U32, name + "_codes")
@@ -106,12 +106,12 @@ def tile_attend_shortvocab_kernel(tc, ht, hd, voc, emb_words, emb_scales, dw, of
             )
             return codes, plane
 
-        def product(lhs, codes, plane, width, name):
+        def product(states, codes, plane, width, name):
             bank = psum.tile([P, width], F32, name=name)
             nc.tensor.matmul_mx(
                 out=bank[:],
-                lhsT=lhs[0][:].bitcast(FP8X4),
-                lhsT_scale=lhs[1][:],
+                lhsT=states[0][:].bitcast(FP8X4),
+                lhsT_scale=states[1][:],
                 rhs=codes.bitcast(FP8X4),
                 rhs_scale=plane,
                 start=True,
@@ -124,54 +124,60 @@ def tile_attend_shortvocab_kernel(tc, ht, hd, voc, emb_words, emb_scales, dw, of
                 out=dst, in0=bank[:], scalar1=-1.0, scalar2=before, op0=ALU.mult, op1=ALU.min, accum_out=low
             )
 
-        def exponentials(dst, neg, low, total):
-            nc.scalar.activation(out=dst, in_=neg, func=ACT.Exp, bias=low, scale=-1.0, accum_out=total)
+        def exponentials(dst, negated, low, total):
+            nc.scalar.activation(out=dst, in_=negated, func=ACT.Exp, bias=low, scale=-1.0, accum_out=total)
 
-        nm = sb([P, n_chunks], F32, "nm")
-        s = voc_raw[last][:, 0, 0:n_chunks]
+        neg_m = sb([P, groups], F32, "neg_m")
+        p_part = voc_raw[last][:, 0, 0:groups]
         p = sb([P, V], F32, "p")
         banks = {}
-        span = [slice(starts[c], starts[c] + WIDTHS[c]) for c in range(n_chunks)]
 
-        def scores(c):
-            codes, plane = quantize(voc_bf[c], WIDTHS[c], "voc%d" % c)
-            banks[c] = product(ht_q, codes[:], plane[:], WIDTHS[c], "a%d" % c)
+        def scores(g):
+            codes, plane = quantize(voc_bf[g], WIDTHS[g], "voc%d" % g)
+            banks[g] = product(ht_q, codes[:], plane[:], WIDTHS[g], "a%d" % g)
 
-        half = I // 2
-        halves = [slice(0, half), slice(half, I)]
-        lists = [slice(0, half // 16), slice(half // 16, I // 16)]
+        half = ENTRIES // 2
+        halves = [slice(0, half), slice(half, ENTRIES)]
+        lists = [slice(h.start // PER_COLUMN, h.stop // PER_COLUMN) for h in halves]
         interleave(nc.scalar.copy, hd_bf[:], hd_raw[:])
         hd_q = quantize(hd_bf, Q, "hd")
-        g_scales = sb([P, I], U8, "g_scales")
+        g_scales = sb([P, ENTRIES], U8, "g_scales")
         nc.vector.tensor_copy(out=g_scales[:], in_=scales[:].indirect(offs_sb[:]))
-        g_words = sb([P, I], U32, "g_words", "scales_then_words")
+        g_words = sb([P, ENTRIES], U32, "g_words", "scales_then_words")
         for h in range(2):
             nc.vector.tensor_copy(out=g_words[:, halves[h]], in_=words[:].indirect(offs_sb[:, lists[h]]))
         b = [product(hd_q, g_words[:, halves[h]], g_scales[:, halves[h]], half, "b%d" % h) for h in range(2)]
-        neg_b = sb([P, I], F32, "neg_b")
+        neg_b = sb([P, ENTRIES], F32, "neg_b")
+
         neg_last = sb([P, WIDTHS[last]], F32, "neg_last")
-        flat = [raw[:].rearrange("p j w -> p (j w)") for raw in voc_raw]
-        neg_a = [neg_b[:, :256], flat[2][:, :512], flat[3][:, :512], flat[4][:, 256:768], neg_last[:]]
-        nb = sb([P, 2], F32, "nb")
-        negate_and_min(neg_b[:, halves[0]], b[0], nb[:, 0:1], None)
-        negate_and_min(neg_b[:, halves[1]], b[1], nb[:, 1:2], nb[:, 0:1])
-        r = sb([P, I], F32, "r")
-        r_sum = sb([P, 1], F32, "r_sum")
-        exponentials(r[:], neg_b[:], nb[:, 1:2], r_sum[:])
+        staged = [raw[:].rearrange("p j w -> p (j w)") for raw in voc_raw]
+        neg_a = [staged[0][:, : WIDTHS[0]]]
+        neg_a += [staged[g + 1][:, : WIDTHS[g]] for g in range(1, last - 1)]
+        neg_a += [staged[last][:, WIDTHS[last] : WIDTHS[last] + WIDTHS[last - 1]], neg_last[:]]
+
+        neg_mb = sb([P, 2], F32, "neg_mb")
+        negate_and_min(neg_b[:, halves[0]], b[0], neg_mb[:, 0:1], None)
+        negate_and_min(neg_b[:, halves[1]], b[1], neg_mb[:, 1:2], neg_mb[:, 0:1])
+
         interleave(nc.scalar.copy, ht_bf[:], ht_raw[:])
         ht_q = quantize(ht_bf, Q, "ht")
-        cast_voc(0, CAST, nc.scalar.copy)
+        interleave_piece(0, nc.scalar.copy)
         scores(0)
+        r = sb([P, ENTRIES], F32, "r", "voc_bf0")
+        r_sum = sb([P, 1], F32, "r_sum")
+        exponentials(r[:], neg_b[:], neg_mb[:, 1:2], r_sum[:])
+        negate_and_min(neg_a[0], banks[0], neg_m[:, 0:1], None)
         nc.vector.tensor_copy(out=rf[:].indirect(offs2_sb[:]), in_=r[:])
-        negate_and_min(neg_a[0], banks[0], nm[:, 0:1], None)
-        for unit in (1, 2, 3, 4, 5, 7):
-            cast_voc(unit * CAST, CAST, nc.scalar.copy)
+
+        for piece in range(1, V // PIECE):
+            if piece != VECTOR_PIECE:
+                interleave_piece(piece, nc.scalar.copy)
         scores(1)
-        cast_voc(6 * CAST, CAST, nc.vector.tensor_copy)
-        for c in range(2, n_chunks):
-            scores(c)
-        for c in range(1, n_chunks):
-            negate_and_min(neg_a[c], banks[c], nm[:, c : c + 1], nm[:, c - 1 : c])
+        interleave_piece(VECTOR_PIECE, nc.vector.tensor_copy)
+        for g in range(2, groups):
+            scores(g)
+        for g in range(1, groups):
+            negate_and_min(neg_a[g], banks[g], neg_m[:, g : g + 1], neg_m[:, g - 1 : g])
 
         r_inv = sb([P, 1], F32, "r_inv", "voc%d_plane" % last)
         nc.vector.reciprocal(out=r_inv[:], in_=r_sum[:])
@@ -180,64 +186,67 @@ def tile_attend_shortvocab_kernel(tc, ht, hd, voc, emb_words, emb_scales, dw, of
             out=neg_c[:], in0=r_inv[:], scalar1=dw_sb[:], scalar2=-1.0, op0=ALU.mult, op1=ALU.mult
         )
 
-        for c in range(last):
-            exponentials(p[:, span[c]], neg_a[c], nm[:, c : c + 1], s[:, c : c + 1])
+        for g in range(last):
+            exponentials(p[:, span[g]], neg_a[g], neg_m[:, g : g + 1], p_part[:, g : g + 1])
         e_raw = sb([P, last], F32, "e_raw")
-        nc.scalar.activation(out=e_raw[:], in_=nm[:, :last], func=ACT.Exp, bias=nm[:, last:], scale=-1.0)
-        exponentials(p[:, span[last]], neg_a[last], nm[:, last:], s[:, last:])
+        nc.scalar.activation(out=e_raw[:], in_=neg_m[:, :last], func=ACT.Exp, bias=neg_m[:, last:], scale=-1.0)
+        exponentials(p[:, span[last]], neg_a[last], neg_m[:, last:], p_part[:, last:])
         nc.vector.tensor_scalar(out=e[:, :last], in0=e_raw[:], scalar1=TINY, scalar2=None, op0=ALU.max)
-        nc.vector.tensor_scalar(
-            out=weight[:, n_chunks:], in0=e_raw[:, last - 1 :], scalar1=TINY, scalar2=None, op0=ALU.max
-        )
-        g = sb([P, last], F32, "g")
-        nc.vector.reciprocal(out=g[:], in_=e[:, :last])
+        e_inv = sb([P, last], F32, "e_inv")
+        nc.vector.reciprocal(out=e_inv[:], in_=e[:, :last])
 
-        es = sb([P, n_chunks], F32, "es")
-        t = sb([P, n_chunks], F32, "t")
+        terms = sb([P, groups], F32, "terms")
+        factor = sb([P, groups], F32, "factor")
         nc.vector.scalar_tensor_tensor(
-            out=es[:], in0=s, scalar=neg_c[:], in1=e[:], op0=ALU.mult, op1=ALU.mult, accum_out=t[:, last:]
+            out=terms[:], in0=p_part, scalar=neg_c[:], in1=e[:, :groups], op0=ALU.mult, op1=ALU.mult,
+            accum_out=factor[:, last:],
         )
-        nc.vector.tensor_scalar(out=t[:, :last], in0=g[:], scalar1=t[:, last:], scalar2=None, op0=ALU.mult)
+        nc.vector.tensor_scalar(
+            out=factor[:, :last], in0=e_inv[:], scalar1=factor[:, last:], scalar2=None, op0=ALU.mult
+        )
 
         d = sb([P, V], F32, "d")
         u = sb([P, V], F32, "u")
         mid = starts[last - 1] + ON_VECTOR
         own = slice(starts[last - 1], mid)
 
-        def differences(c, cols):
+        def differences(g, cols):
             nc.vector.scalar_tensor_tensor(
-                out=d[:, cols], in0=rf[:, cols], scalar=t[:, c : c + 1], in1=p[:, cols], op0=ALU.mult, op1=ALU.add
+                out=d[:, cols], in0=rf[:, cols], scalar=factor[:, g : g + 1], in1=p[:, cols],
+                op0=ALU.mult, op1=ALU.add,
             )
 
-        def positive_parts(c, cols):
+        def positive_parts(g, cols):
             nc.scalar.activation(
-                out=u[:, cols], in_=d[:, cols], func=ACT.Relu, scale=e[:, c : c + 1], accum_out=u_part[:, c : c + 1]
+                out=u[:, cols], in_=d[:, cols], func=ACT.Relu, scale=e[:, g : g + 1],
+                accum_out=u_part[:, g + 1 : g + 2],
             )
 
-        for c in [last] + list(range(last - 1)):
-            differences(c, span[c])
-            positive_parts(c, span[c])
+        for g in [last] + list(range(last - 1)):
+            differences(g, span[g])
+            positive_parts(g, span[g])
         differences(last - 1, own)
         differences(last - 1, slice(mid, starts[last]))
         positive_parts(last - 1, slice(mid, starts[last]))
         nc.vector.tensor_scalar(
             out=u[:, own], in0=d[:, own], scalar1=0.0, scalar2=None, op0=ALU.max, op1=ALU.add,
-            accum_out=u_part[:, n_chunks:],
+            accum_out=u_part[:, 0:1],
         )
-        u_scaled = sb([P, n_chunks + 1], F32, "u_scaled")
-        u_sum = sb([P, 1], F32, "u_sum")
+        u_terms = sb([P, groups + 1], F32, "u_terms")
+        u_mean = sb([P, 1], F32, "u_mean")
         nc.vector.scalar_tensor_tensor(
-            out=u_scaled[:], in0=u_part[:], scalar=1.0 / V, in1=weight[:], op0=ALU.mult, op1=ALU.mult,
-            accum_out=u_sum[:],
+            out=u_terms[:], in0=u_part[:], scalar=1.0 / V, in1=e[:, last - 1 :], op0=ALU.mult, op1=ALU.mult,
+            accum_out=u_mean[:],
         )
-        k = sb([P, 1], F32, "k")
-        nc.vector.reciprocal(out=k[:], in_=u_sum[:])
+        norm = sb([P, 1], F32, "norm")
+        nc.vector.reciprocal(out=norm[:], in_=u_mean[:])
+
         y = sb([P, V], F32, "y")
-        for c in range(last - 1):
-            nc.vector.tensor_scalar(out=y[:, span[c]], in0=u[:, span[c]], scalar1=k[:], scalar2=None, op0=ALU.mult)
-            nc.sync.dma_start(out=out[:, span[c]], in_=y[:, span[c]])
+        for g in range(last - 1):
+            nc.vector.tensor_scalar(out=y[:, span[g]], in0=u[:, span[g]], scalar1=norm[:], scalar2=None, op0=ALU.mult)
+            nc.sync.dma_start(out=out[:, span[g]], in_=y[:, span[g]])
         nc.vector.tensor_scalar(
-            out=y[:, own], in0=u[:, own], scalar1=k[:], scalar2=weight[:, n_chunks:], op0=ALU.mult, op1=ALU.mult
+            out=y[:, own], in0=u[:, own], scalar1=norm[:], scalar2=e[:, last - 1 : last], op0=ALU.mult, op1=ALU.mult
         )
-        nc.vector.tensor_scalar(out=y[:, mid:], in0=u[:, mid:], scalar1=k[:], scalar2=None, op0=ALU.mult)
+        nc.vector.tensor_scalar(out=y[:, mid:], in0=u[:, mid:], scalar1=norm[:], scalar2=None, op0=ALU.mult)
         nc.sync.dma_start(out=out[:, starts[last - 1] :], in_=y[:, starts[last - 1] :])

from contextlib import ExitStack

import concourse.mybir as mybir

F32 = mybir.dt.float32
BF16 = mybir.dt.bfloat16
I32 = mybir.dt.int32
U32 = mybir.dt.uint32
U16 = mybir.dt.uint16
U8 = mybir.dt.uint8
FP8X4 = mybir.dt.float8_e4m3fn_x4
ALU = mybir.AluOpType
ACT = mybir.ActivationFunctionType

P = 128
PACK = 4
Q = 128
V = 2048
T = 2048
ENTRIES = 512
PER_COLUMN = 16
QUADRANT = 32
LINE = 4

WIDTHS = (256, 512, 512, 512, 256)
PIECE = 256
VECTOR_PIECE = V // PIECE - 2
ON_VECTOR = 256
TINY = 1e-26

FLOPS = 2 * P * PACK * Q * (V + ENTRIES)


def interleave(engine_copy, dst, src):
    engine_copy(
        out=dst.rearrange("p (c i) t -> p c t i", i=LINE),
        in_=src.rearrange("p t (c i) -> p c t i", i=LINE),
    )


def tile_attend_shortvocab_kernel(tc, ht, hd, voc, emb_words, emb_scales, dw, offs, offs2, out):
    nc = tc.nc
    groups = len(WIDTHS)
    last = groups - 1
    starts = [sum(WIDTHS[:g]) for g in range(groups)]
    span = [slice(starts[g], starts[g] + WIDTHS[g]) for g in range(groups)]

    with ExitStack() as ctx:
        keep = ctx.enter_context(tc.tile_pool(name="keep", bufs=1))
        psum = ctx.enter_context(tc.psum_pool(name="psum", bufs=1))

        def sb(shape, dtype, name, tag=None):
            return keep.tile(shape, dtype, name=name, tag=tag or name, align_bytes=64)

        offs_sb = sb([P, ENTRIES // PER_COLUMN], U16, "offs_sb")
        offs2_sb = sb([P, ENTRIES // PER_COLUMN], U16, "offs2_sb")
        dw_sb = sb([P, 1], F32, "dw_sb")
        words = sb([P, T], U32, "words")
        scales = sb([P, T], U8, "scales", "scales_then_words")
        hd_raw = sb([P, PACK, Q], F32, "hd_raw")
        ht_raw = sb([P, PACK, Q], F32, "ht_raw")
        voc_raw = [sb([P, PACK, w], F32, "voc_raw%d" % g) for g, w in enumerate(WIDTHS)]
        rf = sb([P, V], F32, "rf")
        zero = sb([P, 1], F32, "zero")
        e = sb([P, 2 * groups - 1], F32, "e")
        u_part = sb([P, groups + 1], F32, "u_part")

        nc.vector.memset(scales[:].bitcast(I32), 0)
        nc.vector.memset(zero[:], 0.0)
        nc.vector.memset(e[:, groups:], 1.0)
        nc.vector.memset(rf[:], 0.0)

        def load_rows(dst, rows):
            nc.sync.dma_start(out=dst[:], in_=rows.rearrange("(p j) w -> p j w", j=PACK))

        nc.sync.dma_start(out=offs_sb[:], in_=offs)
        nc.sync.dma_start(out=offs2_sb[:], in_=offs2)
        load_rows(hd_raw, hd)
        nc.sync.dma_start(out=words[:].bitcast(I32), in_=emb_words[0].rearrange("p n t -> p (n t)").bitcast(I32))
        for quad in range(P // QUADRANT):
            nc.scalar.dma_start(
                out=scales[:].bitcast(I32)[QUADRANT * quad : QUADRANT * quad + 4, :],
                in_=emb_scales[0, 4 * quad : 4 * quad + 4, :].bitcast(I32),
            )
        nc.scalar.activation(out=e[:, last:groups], in_=zero[:], func=ACT.Exp)
        load_rows(voc_raw[0], voc[:, span[0]])
        load_rows(ht_raw, ht)
        for g in range(1, groups):
            load_rows(voc_raw[g], voc[:, span[g]])
        nc.sync.dma_start(out=dw_sb[:], in_=dw)

        hd_bf = sb([P, Q, PACK], BF16, "hd_bf")
        ht_bf = sb([P, Q, PACK], BF16, "ht_bf")
        voc_bf = [sb([P, w, PACK], BF16, "voc_bf%d" % g) for g, w in enumerate(WIDTHS)]

        def interleave_piece(piece, engine_copy):
            g = max(i for i in range(groups) if starts[i] <= piece * PIECE)
            cols = slice(piece * PIECE - starts[g], (piece + 1) * PIECE - starts[g])
            interleave(engine_copy, voc_bf[g][:, cols, :], voc_raw[g][:, :, cols])

        def quantize(src, width, name):
            codes = sb([P, width], U32, name + "_codes")
            plane = sb([P, width], U8, name + "_plane")
            nc.vector.quantize_mx(
                out=codes[:].bitcast(FP8X4), scales=plane[:], in_=src[:].rearrange("p w t -> p (w t)")
            )
            return codes, plane

        def product(states, codes, plane, width, name):
            bank = psum.tile([P, width], F32, name=name)
            nc.tensor.matmul_mx(
                out=bank[:],
                lhsT=states[0][:].bitcast(FP8X4),
                lhsT_scale=states[1][:],
                rhs=codes.bitcast(FP8X4),
                rhs_scale=plane,
                start=True,
                stop=True,
            )
            return bank

        def negate_and_min(dst, bank, low, before):
            nc.vector.tensor_scalar(
                out=dst, in0=bank[:], scalar1=-1.0, scalar2=before, op0=ALU.mult, op1=ALU.min, accum_out=low
            )

        def exponentials(dst, negated, low, total):
            nc.scalar.activation(out=dst, in_=negated, func=ACT.Exp, bias=low, scale=-1.0, accum_out=total)

        neg_m = sb([P, groups], F32, "neg_m")
        p_part = voc_raw[last][:, 0, 0:groups]
        p = sb([P, V], F32, "p")
        banks = {}

        def scores(g):
            codes, plane = quantize(voc_bf[g], WIDTHS[g], "voc%d" % g)
            banks[g] = product(ht_q, codes[:], plane[:], WIDTHS[g], "a%d" % g)

        half = ENTRIES // 2
        halves = [slice(0, half), slice(half, ENTRIES)]
        lists = [slice(h.start // PER_COLUMN, h.stop // PER_COLUMN) for h in halves]
        interleave(nc.scalar.copy, hd_bf[:], hd_raw[:])
        hd_q = quantize(hd_bf, Q, "hd")
        g_scales = sb([P, ENTRIES], U8, "g_scales")
        nc.vector.tensor_copy(out=g_scales[:], in_=scales[:].indirect(offs_sb[:]))
        g_words = sb([P, ENTRIES], U32, "g_words", "scales_then_words")
        for h in range(2):
            nc.vector.tensor_copy(out=g_words[:, halves[h]], in_=words[:].indirect(offs_sb[:, lists[h]]))
        b = [product(hd_q, g_words[:, halves[h]], g_scales[:, halves[h]], half, "b%d" % h) for h in range(2)]
        neg_b = sb([P, ENTRIES], F32, "neg_b")

        neg_last = sb([P, WIDTHS[last]], F32, "neg_last")
        staged = [raw[:].rearrange("p j w -> p (j w)") for raw in voc_raw]
        neg_a = [staged[0][:, : WIDTHS[0]]]
        neg_a += [staged[g + 1][:, : WIDTHS[g]] for g in range(1, last - 1)]
        neg_a += [staged[last][:, WIDTHS[last] : WIDTHS[last] + WIDTHS[last - 1]], neg_last[:]]

        neg_mb = sb([P, 2], F32, "neg_mb")
        negate_and_min(neg_b[:, halves[0]], b[0], neg_mb[:, 0:1], None)
        negate_and_min(neg_b[:, halves[1]], b[1], neg_mb[:, 1:2], neg_mb[:, 0:1])

        interleave(nc.scalar.copy, ht_bf[:], ht_raw[:])
        ht_q = quantize(ht_bf, Q, "ht")
        interleave_piece(0, nc.scalar.copy)
        scores(0)
        r = sb([P, ENTRIES], F32, "r", "voc_bf0")
        r_sum = sb([P, 1], F32, "r_sum")
        exponentials(r[:], neg_b[:], neg_mb[:, 1:2], r_sum[:])
        negate_and_min(neg_a[0], banks[0], neg_m[:, 0:1], None)
        nc.vector.tensor_copy(out=rf[:].indirect(offs2_sb[:]), in_=r[:])

        for piece in range(1, V // PIECE):
            if piece != VECTOR_PIECE:
                interleave_piece(piece, nc.scalar.copy)
        scores(1)
        interleave_piece(VECTOR_PIECE, nc.vector.tensor_copy)
        for g in range(2, groups):
            scores(g)
        for g in range(1, groups):
            negate_and_min(neg_a[g], banks[g], neg_m[:, g : g + 1], neg_m[:, g - 1 : g])

        r_inv = sb([P, 1], F32, "r_inv", "voc%d_plane" % last)
        nc.vector.reciprocal(out=r_inv[:], in_=r_sum[:])
        neg_c = sb([P, 1], F32, "neg_c")
        nc.vector.tensor_scalar(
            out=neg_c[:], in0=r_inv[:], scalar1=dw_sb[:], scalar2=-1.0, op0=ALU.mult, op1=ALU.mult
        )

        for g in range(last):
            exponentials(p[:, span[g]], neg_a[g], neg_m[:, g : g + 1], p_part[:, g : g + 1])
        e_raw = sb([P, last], F32, "e_raw")
        nc.scalar.activation(out=e_raw[:], in_=neg_m[:, :last], func=ACT.Exp, bias=neg_m[:, last:], scale=-1.0)
        exponentials(p[:, span[last]], neg_a[last], neg_m[:, last:], p_part[:, last:])
        nc.vector.tensor_scalar(out=e[:, :last], in0=e_raw[:], scalar1=TINY, scalar2=None, op0=ALU.max)
        e_inv = sb([P, last], F32, "e_inv")
        nc.vector.reciprocal(out=e_inv[:], in_=e[:, :last])

        terms = sb([P, groups], F32, "terms")
        factor = sb([P, groups], F32, "factor")
        nc.vector.scalar_tensor_tensor(
            out=terms[:], in0=p_part, scalar=neg_c[:], in1=e[:, :groups], op0=ALU.mult, op1=ALU.mult,
            accum_out=factor[:, last:],
        )
        nc.vector.tensor_scalar(
            out=factor[:, :last], in0=e_inv[:], scalar1=factor[:, last:], scalar2=None, op0=ALU.mult
        )

        d = sb([P, V], F32, "d")
        u = sb([P, V], F32, "u")
        mid = starts[last - 1] + ON_VECTOR
        own = slice(starts[last - 1], mid)

        def differences(g, cols):
            nc.vector.scalar_tensor_tensor(
                out=d[:, cols], in0=rf[:, cols], scalar=factor[:, g : g + 1], in1=p[:, cols],
                op0=ALU.mult, op1=ALU.add,
            )

        def positive_parts(g, cols):
            nc.scalar.activation(
                out=u[:, cols], in_=d[:, cols], func=ACT.Relu, scale=e[:, g : g + 1],
                accum_out=u_part[:, g + 1 : g + 2],
            )

        for g in [last] + list(range(last - 1)):
            differences(g, span[g])
            positive_parts(g, span[g])
        differences(last - 1, own)
        differences(last - 1, slice(mid, starts[last]))
        positive_parts(last - 1, slice(mid, starts[last]))
        nc.vector.tensor_scalar(
            out=u[:, own], in0=d[:, own], scalar1=0.0, scalar2=None, op0=ALU.max, op1=ALU.add,
            accum_out=u_part[:, 0:1],
        )
        u_terms = sb([P, groups + 1], F32, "u_terms")
        u_mean = sb([P, 1], F32, "u_mean")
        nc.vector.scalar_tensor_tensor(
            out=u_terms[:], in0=u_part[:], scalar=1.0 / V, in1=e[:, last - 1 :], op0=ALU.mult, op1=ALU.mult,
            accum_out=u_mean[:],
        )
        norm = sb([P, 1], F32, "norm")
        nc.vector.reciprocal(out=norm[:], in_=u_mean[:])

        y = sb([P, V], F32, "y")
        for g in range(last - 1):
            nc.vector.tensor_scalar(out=y[:, span[g]], in0=u[:, span[g]], scalar1=norm[:], scalar2=None, op0=ALU.mult)
            nc.sync.dma_start(out=out[:, span[g]], in_=y[:, span[g]])
        nc.vector.tensor_scalar(
            out=y[:, own], in0=u[:, own], scalar1=norm[:], scalar2=e[:, last - 1 : last], op0=ALU.mult, op1=ALU.mult
        )
        nc.vector.tensor_scalar(out=y[:, mid:], in0=u[:, mid:], scalar1=norm[:], scalar2=None, op0=ALU.mult)
        nc.sync.dma_start(out=out[:, starts[last - 1] :], in_=y[:, starts[last - 1] :])
